import numpy as np
import ml_dtypes


def mxq(x, axis, fmt="e4m3"):
    dtype, down = {"e4m3": (ml_dtypes.float8_e4m3fn, 7), "e5m2": (ml_dtypes.float8_e5m2, 14)}[fmt]
    v = np.moveaxis(np.asarray(x, np.float32).astype(ml_dtypes.bfloat16).astype(np.float64), axis, -1)
    blocks = v.reshape(v.shape[:-1] + (-1, 32))
    amax = np.abs(blocks).max(-1, keepdims=True)
    byte = np.maximum(np.where(amax > 0, np.frexp(amax)[1] - 1 + 127, 0) - down, 1)
    scale = np.exp2(byte - 127.0)
    codes = (blocks / scale).astype(np.float32).astype(dtype).astype(np.float64)
    return np.moveaxis((codes * scale).reshape(v.shape), -1, axis)


WIDE = False


def mx_kscale(k):
    if not WIDE:
        return np.ones(k)
    levels = np.array([10, -10, 5, -5, 0])
    if k % 512:
        return np.exp2(np.random.permutation(np.resize(levels, k // 32))).repeat(32)
    a = np.empty((k // 512, 16))
    for p in range(k // 512):
        a[p, :8] = np.random.permutation(np.resize(levels, 8))
        for g in range(8):
            far = levels[np.abs(levels - a[p, g]) >= 10]
            a[p, g + 8] = far[np.random.randint(len(far))]
    return np.exp2(a.ravel()).repeat(32)


def f64(x):
    return np.asarray(x).astype(np.float64)


def striped(idx):
    return np.tile(idx.reshape(-1, 16).T, (8, 1)).astype(np.uint16)


def unstriped(offs):
    return offs[:16].T.reshape(-1).astype(np.int64)


def pack_weight(w):
    k, n = w.shape
    w = f64(np.asarray(w, np.float32).astype(ml_dtypes.bfloat16)).reshape(k // 32, 32, n)
    amax = np.abs(w).max(1)
    byte = np.clip(np.where(amax > 0, np.frexp(amax)[1] - 1 + 127 - 7, 1), 1, 254)
    scaled = (w * np.exp2(127.0 - byte)[:, None, :]).reshape(k, n).astype(np.float32)
    words = np.ascontiguousarray(scaled.reshape(k // 512, 128, 4, n).transpose(0, 1, 3, 2)).astype(ml_dtypes.float8_e4m3fn).view(np.uint8)
    return words, np.ascontiguousarray(byte.astype(np.uint8).reshape(k // 512, 16, n))


def unpack_weight(words, scales):
    g, p, n, _ = words.shape
    vals = np.ascontiguousarray(words).view(ml_dtypes.float8_e4m3fn).astype(np.float64) * np.repeat(np.exp2(scales.astype(np.float64) - 127.0), 8, axis=1)[..., None]
    return vals.transpose(0, 1, 3, 2).reshape(g * 512, n)


K, T, S, N = 512, 1024, 256, 128
P = 2 ** 7


def setup_inputs():
    n = np.random.standard_normal
    s = mx_kscale(K)[:, None]
    packed_xT = pack_weight(n((K, T)) * s)
    return {
        "x_words": packed_xT[0],
        "x_scales": packed_xT[1],
        "w1": (n((K, N)) / np.sqrt(K) / s).astype(np.float32),
        "w2": (n((K, N)) / np.sqrt(K) / s).astype(np.float32),
        "w3": (n((K, N)) / np.sqrt(K) / s).astype(np.float32),
        "w4": (n((K, N)) / np.sqrt(K) / s).astype(np.float32),
        "gl": (np.tile(np.random.uniform(0.2, 1.6, T), (P, 1))).astype(np.float32),
        "gt": (np.tile(np.random.uniform(0.2, 1.6, T), (P, 1))).astype(np.float32),
        "gr": (np.tile(np.random.uniform(0.2, 1.6, T), (P, 1))).astype(np.float32),
        "gb": (np.tile(np.random.uniform(0.2, 1.6, T), (P, 1))).astype(np.float32),
        "offs": striped(np.random.permutation(T)[:S]),
    }


def reference(x_words, x_scales, w1, w2, w3, w4, gl, gt, gr, gb, offs):
    xq = unpack_weight(x_words, x_scales)[:, unstriped(offs)]
    yl = mxq(f64(w1), 0, "e4m3").T @ xq
    pl = np.log(np.exp(yl) + 1.0)
    yr = mxq(f64(w3), 0, "e4m3").T @ xq
    pr = np.log(np.exp(yr) + 1.0)
    yt = mxq(f64(w2), 0, "e4m3").T @ xq
    pt = np.log(np.exp(yt) + 1.0)
    yb = mxq(f64(w4), 0, "e4m3").T @ xq
    pb = np.log(np.exp(yb) + 1.0)
    isec = (np.minimum(pl, f64(gl)[:1][:, unstriped(offs)]) + np.minimum(pr, f64(gr)[:1][:, unstriped(offs)])) * (np.minimum(pt, f64(gt)[:1][:, unstriped(offs)]) + np.minimum(pb, f64(gb)[:1][:, unstriped(offs)]))
    uni = (pl + pr) * (pt + pb) + (f64(gl)[:1][:, unstriped(offs)] + f64(gr)[:1][:, unstriped(offs)]) * (f64(gt)[:1][:, unstriped(offs)] + f64(gb)[:1][:, unstriped(offs)]) - isec
    iou = isec / uni
    ew = np.maximum(pl, f64(gl)[:1][:, unstriped(offs)]) + np.maximum(pr, f64(gr)[:1][:, unstriped(offs)])
    eh = np.maximum(pt, f64(gt)[:1][:, unstriped(offs)]) + np.maximum(pb, f64(gb)[:1][:, unstriped(offs)])
    enc = ew * eh
    return -1.0 * iou + 1.0 + (enc - uni) / enc

@@ -1,0 +1,163 @@
+from contextlib import ExitStack
+
+import concourse.mybir as mybir
+from concourse.masks import make_identity
+
+K, T, S, N = 512, 1024, 256, 128
+FLOPS = 4 * 2 * K * S * N
+BYTES = K * T + 16 * T + 4 * K * N * 4 + 4 * T * 4 + 128 * 16 * 2 + N * S * 4
+
+F32 = mybir.dt.float32
+BF16 = mybir.dt.bfloat16
+I32 = mybir.dt.int32
+U32 = mybir.dt.uint32
+U16 = mybir.dt.uint16
+U8 = mybir.dt.uint8
+FP8X4 = mybir.dt.float8_e4m3fn_x4
+ALU = mybir.AluOpType
+ACT = mybir.ActivationFunctionType
+
+P = 128
+HALVES = S // P
+EXP_CAP = 2.0 ** 60
+ROW_STEP = 4
+
+
+def tile_picked_ygiou_giou_p_kernel(
+    tc, x_words, x_scales, w1, w2, w3, w4, gl, gt, gr, gb, offs, out
+):
+    nc = tc.nc
+    weights = (w1, w2, w3, w4)
+    truths = (gl, gt, gr, gb)
+    with ExitStack() as ctx:
+        sb = ctx.enter_context(tc.tile_pool(name="sb", bufs=1))
+        ps = ctx.enter_context(tc.psum_pool(name="ps", bufs=1))
+
+        offsets = sb.tile([P, S // 16], U16, name="offsets")
+        word_table = sb.tile([P, T], I32, name="word_table", align_bytes=64)
+        scale_table = sb.tile([P, T], U8, name="scale_table", align_bytes=64)
+        truth_table = sb.tile([P, T], F32, name="truth_table", align_bytes=64)
+        ident = sb.tile([P, P], F32, name="ident", align_bytes=64)
+
+        nc.vector.memset(scale_table[:].bitcast(I32), 0)
+        nc.vector.memset(truth_table[:], 0.0)
+        make_identity(nc, ident[:])
+
+        nc.sync.dma_start(offsets[:], offs)
+        nc.sync.dma_start(word_table[:], x_words[0].rearrange("p n t -> p (n t)").bitcast(I32))
+        for q in range(4):
+            nc.sync.dma_start(
+                scale_table[32 * q : 32 * q + 4, :].bitcast(I32), x_scales[0, 4 * q : 4 * q + 4, :].bitcast(I32)
+            )
+        raw = [sb.tile([P, 4, N], F32, name=f"raw{s}", align_bytes=64) for s in range(4)]
+        for s in range(4):
+            nc.sync.dma_start(raw[s][:], weights[s].rearrange("(p t) m -> p t m", t=4))
+        for s in range(4):
+            nc.sync.dma_start(truth_table[ROW_STEP * s : ROW_STEP * s + 1, :], truths[s][0:1, :])
+
+        x_codes = sb.tile([P, S], U32, name="x_codes", align_bytes=64)
+        x_bytes = sb.tile([P, S], U8, name="x_bytes", align_bytes=64)
+        nc.vector.tensor_copy(x_codes[:], word_table[:].bitcast(U32).indirect(offsets[:]))
+        nc.vector.tensor_copy(x_bytes[:], scale_table[:].indirect(offsets[:]))
+
+        expo = sb.tile([P, 4, S], F32, name="expo", align_bytes=64)
+        logits = []
+        for s in range(4):
+            grouped = sb.tile([P, N, 4], BF16, name=f"grouped{s}", align_bytes=64)
+            dst = grouped[:].rearrange("p (c i) t -> p c t i", i=4)
+            src = raw[s][:].rearrange("p t (c i) -> p c t i", i=4)
+            if s < 2:
+                nc.scalar.activation(dst, src, ACT.Copy)
+            else:
+                nc.vector.tensor_copy(dst, src)
+            w_codes = sb.tile([P, N], U32, name=f"w_codes{s}", align_bytes=64)
+            w_bytes = sb.tile([P, N], U8, name=f"w_bytes{s}", align_bytes=64)
+            nc.vector.quantize_mx(
+                out=w_codes[:].bitcast(FP8X4), scales=w_bytes[:], in_=grouped[:].rearrange("p m t -> p (m t)")
+            )
+            y = ps.tile([P, S], F32, name=f"y{s}")
+            for h in range(HALVES):
+                cols = slice(h * P, (h + 1) * P)
+                nc.tensor.matmul_mx(
+                    out=y[:, cols],
+                    lhsT=x_codes[:, cols].bitcast(FP8X4),
+                    lhsT_scale=x_bytes[:, cols],
+                    rhs=w_codes[:].bitcast(FP8X4),
+                    rhs_scale=w_bytes[:],
+                    start=True,
+                    stop=True,
+                )
+            nc.scalar.activation(expo[:, s, :], y[:], ACT.Exp)
+            logits.append(y)
+
+        capped = sb.tile([P, 4, S], F32, name="capped", align_bytes=64)
+        nc.vector.tensor_scalar(
+            capped[:].rearrange("p s j -> p (s j)"), expo[:].rearrange("p s j -> p (s j)"), EXP_CAP, None, ALU.min
+        )
+
+        picked = sb.tile([P, S], F32, name="picked", align_bytes=64)
+        nc.vector.tensor_copy(picked[:], truth_table[:].indirect(offsets[:]))
+        turned = ps.tile([P, HALVES, P], F32, name="turned")
+        for h in range(HALVES):
+            nc.tensor.transpose(turned[:, h, :], picked[:, h * P : (h + 1) * P], ident[:])
+        g = sb.tile([P, HALVES, 4], F32, name="g")
+        nc.vector.tensor_copy(g[:], turned[:, :, 0 : 4 * ROW_STEP : ROW_STEP])
+        g_sum = sb.tile([P, HALVES, 2], F32, name="g_sum")
+        nc.vector.tensor_tensor(g_sum[:], g[:, :, 0:2], g[:, :, 2:4], ALU.add)
+        g_area = sb.tile([P, HALVES], F32, name="g_area")
+        nc.vector.tensor_tensor(g_area[:], g_sum[:, :, 0], g_sum[:, :, 1], ALU.mult)
+
+        pred = {}
+        spans = {}
+        for axis in range(2):
+            for s in (axis, axis + 2):
+                soft = sb.tile([P, S], F32, name=f"soft{s}", align_bytes=64)
+                nc.scalar.activation(soft[:], capped[:, s, :], ACT.Ln, bias=1.0)
+                pred[s] = sb.tile([P, S], F32, name=f"pred{s}", align_bytes=64)
+                nc.vector.tensor_tensor(pred[s][:], logits[s][:], soft[:], ALU.max)
+            near, far = axis, axis + 2
+            low = {}
+            for h in range(HALVES):
+                cols = slice(h * P, (h + 1) * P)
+                spans[h, axis] = sb.tile([P, 3, P], F32, name=f"spans{h}{axis}", align_bytes=64)
+                low[h] = sb.tile([P, P], F32, name=f"low{h}{axis}", align_bytes=64)
+                nc.vector.tensor_scalar(low[h][:], pred[far][:, cols], g[:, h, far : far + 1], None, ALU.min)
+                nc.vector.tensor_tensor(spans[h, axis][:, 1, :], pred[near][:, cols], pred[far][:, cols], ALU.add)
+            for h in range(HALVES):
+                cols = slice(h * P, (h + 1) * P)
+                nc.vector.scalar_tensor_tensor(
+                    spans[h, axis][:, 0, :], pred[near][:, cols], g[:, h, near : near + 1], low[h][:], ALU.min, ALU.add
+                )
+            for h in range(HALVES):
+                nc.vector.scalar_tensor_tensor(
+                    spans[h, axis][:, 2, :],
+                    spans[h, axis][:, 1, :],
+                    g_sum[:, h, axis : axis + 1],
+                    spans[h, axis][:, 0, :],
+                    ALU.add,
+                    ALU.subtract,
+                )
+
+        areas = {}
+        for h in range(HALVES):
+            areas[h] = sb.tile([P, 3, P], F32, name=f"areas{h}", align_bytes=64)
+            nc.vector.tensor_tensor(areas[h][:], spans[h, 0][:], spans[h, 1][:], ALU.mult)
+        for h in range(HALVES):
+            nc.vector.scalar_tensor_tensor(
+                areas[h][:, 1, :], areas[h][:, 1, :], g_area[:, h : h + 1], areas[h][:, 0, :], ALU.add, ALU.subtract
+            )
+        for h in range(HALVES):
+            root = sb.tile([P, 2, P], F32, name=f"root{h}", align_bytes=64)
+            nc.scalar.activation(root[:], areas[h][:, 1:3, :], ACT.Abs_reciprocal_sqrt)
+            recip = sb.tile([P, 2, P], F32, name=f"recip{h}", align_bytes=64)
+            nc.scalar.activation(recip[:], root[:], ACT.Square)
+            ratio = sb.tile([P, 2, P], F32, name=f"ratio{h}", align_bytes=64)
+            nc.vector.tensor_tensor(ratio[:], areas[h][:, 0:2, :], recip[:], ALU.mult)
+            total = ps.tile([P, P], F32, name=f"total{h}")
+            for term in range(2):
+                nc.tensor.matmul(
+                    total[:], lhsT=ratio[:, term, :], rhs=ident[:], is_transpose=True, start=term == 0, stop=term == 1
+                )
+            loss = sb.tile([P, P], F32, name=f"loss{h}", align_bytes=64)
+            nc.vector.tensor_scalar(loss[:], total[:], -1.0, 2.0, ALU.mult, ALU.add)
+            nc.sync.dma_start(out[:, h * P : (h + 1) * P], loss[:])

@@ -21,6 +21,8 @@ P = 128
 HALVES = S // P
 EXP_CAP = 2.0 ** 60
 ROW_STEP = 4
+SCALAR_CASTS = 2
+SIDE_ORDER = (0, 2, 1, 3)
 
 
 def tile_picked_ygiou_giou_p_kernel(
@@ -36,11 +38,11 @@ def tile_picked_ygiou_giou_p_kernel(
         offsets = sb.tile([P, S // 16], U16, name="offsets")
         word_table = sb.tile([P, T], I32, name="word_table", align_bytes=64)
         scale_table = sb.tile([P, T], U8, name="scale_table", align_bytes=64)
-        truth_table = sb.tile([P, T], F32, name="truth_table", align_bytes=64)
+        truth_table = sb.tile([P, T], F32, name="truth_table", tag="wide", align_bytes=64)
         ident = sb.tile([P, P], F32, name="ident", align_bytes=64)
 
         nc.vector.memset(scale_table[:].bitcast(I32), 0)
-        nc.vector.memset(truth_table[:], 0.0)
+        nc.vector.memset(truth_table[:].bitcast(I32), 0)
         make_identity(nc, ident[:])
 
         nc.sync.dma_start(offsets[:], offs)
@@ -50,7 +52,7 @@ def tile_picked_ygiou_giou_p_kernel(
                 scale_table[32 * q : 32 * q + 4, :].bitcast(I32), x_scales[0, 4 * q : 4 * q + 4, :].bitcast(I32)
             )
         raw = [sb.tile([P, 4, N], F32, name=f"raw{s}", align_bytes=64) for s in range(4)]
-        for s in range(4):
+        for s in SIDE_ORDER:
             nc.sync.dma_start(raw[s][:], weights[s].rearrange("(p t) m -> p t m", t=4))
         for s in range(4):
             nc.sync.dma_start(truth_table[ROW_STEP * s : ROW_STEP * s + 1, :], truths[s][0:1, :])
@@ -60,13 +62,13 @@ def tile_picked_ygiou_giou_p_kernel(
         nc.vector.tensor_copy(x_codes[:], word_table[:].bitcast(U32).indirect(offsets[:]))
         nc.vector.tensor_copy(x_bytes[:], scale_table[:].indirect(offsets[:]))
 
-        expo = sb.tile([P, 4, S], F32, name="expo", align_bytes=64)
-        logits = []
-        for s in range(4):
-            grouped = sb.tile([P, N, 4], BF16, name=f"grouped{s}", align_bytes=64)
+        logits = [[ps.tile([P, 2, N], F32, name=f"logits{h}{end}") for end in range(2)] for h in range(HALVES)]
+        expo = [sb.tile([P, 4, N], F32, name=f"expo{h}", align_bytes=64) for h in range(HALVES)]
+        for turn, s in enumerate(SIDE_ORDER):
+            grouped = sb.tile([P, N, 4], BF16, name=f"grouped{s}", tag=f"stage{turn % 2}", align_bytes=64)
             dst = grouped[:].rearrange("p (c i) t -> p c t i", i=4)
             src = raw[s][:].rearrange("p t (c i) -> p c t i", i=4)
-            if s < 2:
+            if turn < SCALAR_CASTS:
                 nc.scalar.activation(dst, src, ACT.Copy)
             else:
                 nc.vector.tensor_copy(dst, src)
@@ -75,11 +77,10 @@ def tile_picked_ygiou_giou_p_kernel(
             nc.vector.quantize_mx(
                 out=w_codes[:].bitcast(FP8X4), scales=w_bytes[:], in_=grouped[:].rearrange("p m t -> p (m t)")
             )
-            y = ps.tile([P, S], F32, name=f"y{s}")
             for h in range(HALVES):
                 cols = slice(h * P, (h + 1) * P)
                 nc.tensor.matmul_mx(
-                    out=y[:, cols],
+                    out=logits[h][s // 2][:, s % 2, :],
                     lhsT=x_codes[:, cols].bitcast(FP8X4),
                     lhsT_scale=x_bytes[:, cols],
                     rhs=w_codes[:].bitcast(FP8X4),
@@ -87,19 +88,18 @@ def tile_picked_ygiou_giou_p_kernel(
                     start=True,
                     stop=True,
                 )
-            nc.scalar.activation(expo[:, s, :], y[:], ACT.Exp)
-            logits.append(y)
+                nc.scalar.activation(expo[h][:, s, :], logits[h][s // 2][:, s % 2, :], ACT.Exp)
 
-        capped = sb.tile([P, 4, S], F32, name="capped", align_bytes=64)
-        nc.vector.tensor_scalar(
-            capped[:].rearrange("p s j -> p (s j)"), expo[:].rearrange("p s j -> p (s j)"), EXP_CAP, None, ALU.min
-        )
-
-        picked = sb.tile([P, S], F32, name="picked", align_bytes=64)
+        picked = sb.tile([P, S], F32, name="picked", tag="stage1", align_bytes=64)
         nc.vector.tensor_copy(picked[:], truth_table[:].indirect(offsets[:]))
         turned = ps.tile([P, HALVES, P], F32, name="turned")
         for h in range(HALVES):
             nc.tensor.transpose(turned[:, h, :], picked[:, h * P : (h + 1) * P], ident[:])
+
+        capped = sb.tile([P, HALVES, 4, N], F32, name="capped", tag="wide", align_bytes=64)
+        for h in range(HALVES):
+            nc.vector.tensor_scalar(capped[:, h], expo[h][:], EXP_CAP, None, ALU.min)
+
         g = sb.tile([P, HALVES, 4], F32, name="g")
         nc.vector.tensor_copy(g[:], turned[:, :, 0 : 4 * ROW_STEP : ROW_STEP])
         g_sum = sb.tile([P, HALVES, 2], F32, name="g_sum")
@@ -107,57 +107,56 @@ def tile_picked_ygiou_giou_p_kernel(
         g_area = sb.tile([P, HALVES], F32, name="g_area")
         nc.vector.tensor_tensor(g_area[:], g_sum[:, :, 0], g_sum[:, :, 1], ALU.mult)
 
-        pred = {}
-        spans = {}
-        for axis in range(2):
-            for s in (axis, axis + 2):
-                soft = sb.tile([P, S], F32, name=f"soft{s}", align_bytes=64)
-                nc.scalar.activation(soft[:], capped[:, s, :], ACT.Ln, bias=1.0)
-                pred[s] = sb.tile([P, S], F32, name=f"pred{s}", align_bytes=64)
-                nc.vector.tensor_tensor(pred[s][:], logits[s][:], soft[:], ALU.max)
-            near, far = axis, axis + 2
-            low = {}
-            for h in range(HALVES):
-                cols = slice(h * P, (h + 1) * P)
-                spans[h, axis] = sb.tile([P, 3, P], F32, name=f"spans{h}{axis}", align_bytes=64)
-                low[h] = sb.tile([P, P], F32, name=f"low{h}{axis}", align_bytes=64)
-                nc.vector.tensor_scalar(low[h][:], pred[far][:, cols], g[:, h, far : far + 1], None, ALU.min)
-                nc.vector.tensor_tensor(spans[h, axis][:, 1, :], pred[near][:, cols], pred[far][:, cols], ALU.add)
-            for h in range(HALVES):
-                cols = slice(h * P, (h + 1) * P)
-                nc.vector.scalar_tensor_tensor(
-                    spans[h, axis][:, 0, :], pred[near][:, cols], g[:, h, near : near + 1], low[h][:], ALU.min, ALU.add
+        near, far = slice(0, 2), slice(2, 4)
+        soft = [sb.tile([P, 4, N], F32, name=f"soft{h}", align_bytes=64) for h in range(HALVES)]
+        for h in range(HALVES):
+            for pair in (far, near):
+                nc.scalar.activation(soft[h][:, pair, :], capped[:, h, pair, :], ACT.Ln, bias=1.0)
+
+        for h in range(HALVES):
+            pred = sb.tile([P, 4, N], F32, name=f"pred{h}", align_bytes=64)
+            low = sb.tile([P, 2, N], F32, name=f"low{h}", align_bytes=64)
+            spans = sb.tile([P, 3, 2, N], F32, name=f"spans{h}", align_bytes=64)
+            areas = sb.tile([P, 3, N], F32, name=f"areas{h}", align_bytes=64)
+            nc.vector.tensor_tensor(pred[:, far, :], logits[h][1][:], soft[h][:, far, :], ALU.max)
+            nc.vector.tensor_tensor(pred[:, near, :], logits[h][0][:], soft[h][:, near, :], ALU.max)
+            for axis in range(2):
+                nc.vector.tensor_scalar(
+                    low[:, axis, :], pred[:, 2 + axis, :], g[:, h, 2 + axis : 3 + axis], None, ALU.min
                 )
-            for h in range(HALVES):
+            nc.vector.tensor_tensor(spans[:, 1], pred[:, near, :], pred[:, far, :], ALU.add)
+            for axis in range(2):
                 nc.vector.scalar_tensor_tensor(
-                    spans[h, axis][:, 2, :],
-                    spans[h, axis][:, 1, :],
+                    spans[:, 0, axis, :], pred[:, axis, :], g[:, h, axis : axis + 1], low[:, axis, :], ALU.min, ALU.add
+                )
+            for axis in range(2):
+                nc.vector.scalar_tensor_tensor(
+                    spans[:, 2, axis, :],
+                    spans[:, 1, axis, :],
                     g_sum[:, h, axis : axis + 1],
-                    spans[h, axis][:, 0, :],
+                    spans[:, 0, axis, :],
                     ALU.add,
                     ALU.subtract,
                 )
-
-        areas = {}
-        for h in range(HALVES):
-            areas[h] = sb.tile([P, 3, P], F32, name=f"areas{h}", align_bytes=64)
-            nc.vector.tensor_tensor(areas[h][:], spans[h, 0][:], spans[h, 1][:], ALU.mult)
-        for h in range(HALVES):
+            nc.vector.tensor_tensor(areas[:, 0:2, :], spans[:, 0:2, 0, :], spans[:, 0:2, 1, :], ALU.mult)
+            nc.vector.tensor_tensor(areas[:, 2, :], spans[:, 2, 0, :], spans[:, 2, 1, :], ALU.mult)
             nc.vector.scalar_tensor_tensor(
-                areas[h][:, 1, :], areas[h][:, 1, :], g_area[:, h : h + 1], areas[h][:, 0, :], ALU.add, ALU.subtract
+                areas[:, 1, :], areas[:, 1, :], g_area[:, h : h + 1], areas[:, 0, :], ALU.add, ALU.subtract
             )
-        for h in range(HALVES):
-            root = sb.tile([P, 2, P], F32, name=f"root{h}", align_bytes=64)
-            nc.scalar.activation(root[:], areas[h][:, 1:3, :], ACT.Abs_reciprocal_sqrt)
-            recip = sb.tile([P, 2, P], F32, name=f"recip{h}", align_bytes=64)
-            nc.scalar.activation(recip[:], root[:], ACT.Square)
-            ratio = sb.tile([P, 2, P], F32, name=f"ratio{h}", align_bytes=64)
-            nc.vector.tensor_tensor(ratio[:], areas[h][:, 0:2, :], recip[:], ALU.mult)
+
+            root = sb.tile([P, 2, N], F32, name=f"root{h}", align_bytes=64)
+            recip = sb.tile([P, 2, N], F32, name=f"recip{h}", align_bytes=64)
+            ratio = sb.tile([P, 2, N], F32, name=f"ratio{h}", align_bytes=64)
             total = ps.tile([P, P], F32, name=f"total{h}")
-            for term in range(2):
+            for term in (1, 0):
+                nc.scalar.activation(root[:, term, :], areas[:, term + 1, :], ACT.Abs_reciprocal_sqrt)
+            for term in (1, 0):
+                nc.scalar.activation(recip[:, term, :], root[:, term, :], ACT.Square)
+            for term in (1, 0):
+                nc.vector.tensor_tensor(ratio[:, term, :], areas[:, term, :], recip[:, term, :], ALU.mult)
                 nc.tensor.matmul(
-                    total[:], lhsT=ratio[:, term, :], rhs=ident[:], is_transpose=True, start=term == 0, stop=term == 1
+                    total[:], lhsT=ratio[:, term, :], rhs=ident[:], is_transpose=True, start=term == 1, stop=term == 0
                 )
             loss = sb.tile([P, P], F32, name=f"loss{h}", align_bytes=64)
-            nc.vector.tensor_scalar(loss[:], total[:], -1.0, 2.0, ALU.mult, ALU.add)
+            nc.scalar.activation(loss[:], total[:], ACT.Copy, bias=2.0, scale=-1.0)
             nc.sync.dma_start(out[:, h * P : (h + 1) * P], loss[:])

@@ -107,28 +107,54 @@ def tile_picked_ygiou_giou_p_kernel(
         g_area = sb.tile([P, HALVES], F32, name="g_area")
         nc.vector.tensor_tensor(g_area[:], g_sum[:, :, 0], g_sum[:, :, 1], ALU.mult)
 
-        near, far = slice(0, 2), slice(2, 4)
         soft = [sb.tile([P, 4, N], F32, name=f"soft{h}", align_bytes=64) for h in range(HALVES)]
+        pred = [sb.tile([P, 4, N], F32, name=f"pred{h}", align_bytes=64) for h in range(HALVES)]
+        low = [sb.tile([P, 2, N], F32, name=f"low{h}", align_bytes=64) for h in range(HALVES)]
         for h in range(HALVES):
-            for pair in (far, near):
+            for end in (1, 0):
+                pair = slice(2 * end, 2 * end + 2)
                 nc.scalar.activation(soft[h][:, pair, :], capped[:, h, pair, :], ACT.Ln, bias=1.0)
 
+        union, hull, overlap = [], [], []
         for h in range(HALVES):
-            pred = sb.tile([P, 4, N], F32, name=f"pred{h}", align_bytes=64)
-            low = sb.tile([P, 2, N], F32, name=f"low{h}", align_bytes=64)
+            for end in (1, 0):
+                pair = slice(2 * end, 2 * end + 2)
+                nc.vector.tensor_tensor(pred[h][:, pair, :], logits[h][end][:], soft[h][:, pair, :], ALU.max)
+                if end == 1:
+                    for axis in range(2):
+                        nc.vector.tensor_scalar(
+                            low[h][:, axis, :], pred[h][:, 2 + axis, :], g[:, h, 2 + axis : 3 + axis], None, ALU.min
+                        )
             spans = sb.tile([P, 3, 2, N], F32, name=f"spans{h}", align_bytes=64)
             areas = sb.tile([P, 3, N], F32, name=f"areas{h}", align_bytes=64)
-            nc.vector.tensor_tensor(pred[:, far, :], logits[h][1][:], soft[h][:, far, :], ALU.max)
-            nc.vector.tensor_tensor(pred[:, near, :], logits[h][0][:], soft[h][:, near, :], ALU.max)
-            for axis in range(2):
-                nc.vector.tensor_scalar(
-                    low[:, axis, :], pred[:, 2 + axis, :], g[:, h, 2 + axis : 3 + axis], None, ALU.min
-                )
-            nc.vector.tensor_tensor(spans[:, 1], pred[:, near, :], pred[:, far, :], ALU.add)
+            union.append(ps.tile([P, P], F32, name=f"union{h}"))
+            hull.append(ps.tile([P, P], F32, name=f"hull{h}", tag=f"logits{h}1"))
+            overlap.append(ps.tile([P, P], F32, name=f"overlap{h}", tag=f"logits{h}0"))
+            nc.tensor.matmul(
+                union[h][:],
+                lhsT=g_area[:, h : h + 1].to_broadcast([P, P]),
+                rhs=ident[:],
+                is_transpose=True,
+                start=True,
+                stop=False,
+            )
+            nc.vector.tensor_tensor(spans[:, 1], pred[h][:, 0:2, :], pred[h][:, 2:4, :], ALU.add)
             for axis in range(2):
                 nc.vector.scalar_tensor_tensor(
-                    spans[:, 0, axis, :], pred[:, axis, :], g[:, h, axis : axis + 1], low[:, axis, :], ALU.min, ALU.add
+                    spans[:, 0, axis, :],
+                    pred[h][:, axis, :],
+                    g[:, h, axis : axis + 1],
+                    low[h][:, axis, :],
+                    ALU.min,
+                    ALU.add,
                 )
+            nc.vector.tensor_tensor(areas[:, 1, :], spans[:, 1, 0, :], spans[:, 1, 1, :], ALU.mult)
+            nc.tensor.matmul(union[h][:], lhsT=areas[:, 1, :], rhs=ident[:], is_transpose=True, start=False, stop=False)
+            nc.vector.scalar_tensor_tensor(
+                areas[:, 0, :], spans[:, 0, 0, :], -1.0, spans[:, 0, 1, :], ALU.mult, ALU.mult
+            )
+            nc.tensor.matmul(union[h][:], lhsT=areas[:, 0, :], rhs=ident[:], is_transpose=True, start=False, stop=True)
+            nc.tensor.transpose(overlap[h][:], areas[:, 0, :], ident[:])
             for axis in range(2):
                 nc.vector.scalar_tensor_tensor(
                     spans[:, 2, axis, :],
@@ -138,25 +164,19 @@ def tile_picked_ygiou_giou_p_kernel(
                     ALU.add,
                     ALU.subtract,
                 )
-            nc.vector.tensor_tensor(areas[:, 0:2, :], spans[:, 0:2, 0, :], spans[:, 0:2, 1, :], ALU.mult)
             nc.vector.tensor_tensor(areas[:, 2, :], spans[:, 2, 0, :], spans[:, 2, 1, :], ALU.mult)
-            nc.vector.scalar_tensor_tensor(
-                areas[:, 1, :], areas[:, 1, :], g_area[:, h : h + 1], areas[:, 0, :], ALU.add, ALU.subtract
-            )
+            nc.tensor.transpose(hull[h][:], areas[:, 2, :], ident[:])
 
-            root = sb.tile([P, 2, N], F32, name=f"root{h}", align_bytes=64)
-            recip = sb.tile([P, 2, N], F32, name=f"recip{h}", align_bytes=64)
-            ratio = sb.tile([P, 2, N], F32, name=f"ratio{h}", align_bytes=64)
-            total = ps.tile([P, P], F32, name=f"total{h}")
-            for term in (1, 0):
-                nc.scalar.activation(root[:, term, :], areas[:, term + 1, :], ACT.Abs_reciprocal_sqrt)
-            for term in (1, 0):
-                nc.scalar.activation(recip[:, term, :], root[:, term, :], ACT.Square)
-            for term in (1, 0):
-                nc.vector.tensor_tensor(ratio[:, term, :], areas[:, term, :], recip[:, term, :], ALU.mult)
-                nc.tensor.matmul(
-                    total[:], lhsT=ratio[:, term, :], rhs=ident[:], is_transpose=True, start=term == 1, stop=term == 0
-                )
+        ratio = sb.tile([P, HALVES, 2, P], F32, name="ratio", tag="spans1", align_bytes=64)
+        for h in range(HALVES):
+            root = sb.tile([P, 2, P], F32, name=f"root{h}", align_bytes=64)
+            recip = sb.tile([P, 2, P], F32, name=f"recip{h}", align_bytes=64)
+            nc.scalar.activation(root[:, 0, :], union[h][:], ACT.Abs_reciprocal_sqrt)
+            nc.scalar.activation(recip[:, 0, :], root[:, 0, :], ACT.Square)
+            nc.scalar.activation(root[:, 1, :], hull[h][:], ACT.Abs_reciprocal_sqrt)
+            nc.scalar.activation(recip[:, 1, :], root[:, 1, :], ACT.Square)
+            nc.vector.tensor_tensor(ratio[:, h, 0, :], overlap[h][:], recip[:, 0, :], ALU.mult)
+            nc.vector.scalar_tensor_tensor(ratio[:, h, 1, :], union[h][:], -1.0, recip[:, 1, :], ALU.mult, ALU.mult)
             loss = sb.tile([P, P], F32, name=f"loss{h}", align_bytes=64)
-            nc.scalar.activation(loss[:], total[:], ACT.Copy, bias=2.0, scale=-1.0)
+            nc.vector.scalar_tensor_tensor(loss[:], ratio[:, h, 1, :], 2.0, ratio[:, h, 0, :], ALU.add, ALU.add)
             nc.sync.dma_start(out[:, h * P : (h + 1) * P], loss[:])

from contextlib import ExitStack

import concourse.mybir as mybir
from concourse.masks import make_identity

K, T, S, N = 512, 1024, 256, 128
FLOPS = 4 * 2 * K * S * N
BYTES = K * T + 16 * T + 4 * K * N * 4 + 4 * T * 4 + 128 * 16 * 2 + N * S * 4

F32 = mybir.dt.float32
BF16 = mybir.dt.bfloat16
I32 = mybir.dt.int32
U32 = mybir.dt.uint32
U16 = mybir.dt.uint16
U8 = mybir.dt.uint8
FP8X4 = mybir.dt.float8_e4m3fn_x4
ALU = mybir.AluOpType
ACT = mybir.ActivationFunctionType

P = 128
HALVES = S // P
EXP_CAP = 2.0 ** 60
ROW_STEP = 4
SCALAR_CASTS = 2
SIDE_ORDER = (0, 2, 1, 3)


def tile_picked_ygiou_giou_p_kernel(
    tc, x_words, x_scales, w1, w2, w3, w4, gl, gt, gr, gb, offs, out
):
    nc = tc.nc
    weights = (w1, w2, w3, w4)
    truths = (gl, gt, gr, gb)
    with ExitStack() as ctx:
        sb = ctx.enter_context(tc.tile_pool(name="sb", bufs=1))
        ps = ctx.enter_context(tc.psum_pool(name="ps", bufs=1))

        offsets = sb.tile([P, S // 16], U16, name="offsets")
        word_table = sb.tile([P, T], I32, name="word_table", align_bytes=64)
        scale_table = sb.tile([P, T], U8, name="scale_table", align_bytes=64)
        truth_table = sb.tile([P, T], F32, name="truth_table", tag="wide", align_bytes=64)
        ident = sb.tile([P, P], F32, name="ident", align_bytes=64)

        nc.vector.memset(scale_table[:].bitcast(I32), 0)
        nc.vector.memset(truth_table[:].bitcast(I32), 0)
        make_identity(nc, ident[:])

        nc.sync.dma_start(offsets[:], offs)
        nc.sync.dma_start(word_table[:], x_words[0].rearrange("p n t -> p (n t)").bitcast(I32))
        for q in range(4):
            nc.sync.dma_start(
                scale_table[32 * q : 32 * q + 4, :].bitcast(I32), x_scales[0, 4 * q : 4 * q + 4, :].bitcast(I32)
            )
        raw = [sb.tile([P, 4, N], F32, name=f"raw{s}", align_bytes=64) for s in range(4)]
        for s in SIDE_ORDER:
            nc.sync.dma_start(raw[s][:], weights[s].rearrange("(p t) m -> p t m", t=4))
        for s in range(4):
            nc.sync.dma_start(truth_table[ROW_STEP * s : ROW_STEP * s + 1, :], truths[s][0:1, :])

        x_codes = sb.tile([P, S], U32, name="x_codes", align_bytes=64)
        x_bytes = sb.tile([P, S], U8, name="x_bytes", align_bytes=64)
        nc.vector.tensor_copy(x_codes[:], word_table[:].bitcast(U32).indirect(offsets[:]))
        nc.vector.tensor_copy(x_bytes[:], scale_table[:].indirect(offsets[:]))

        logits = [[ps.tile([P, 2, N], F32, name=f"logits{h}{end}") for end in range(2)] for h in range(HALVES)]
        expo = [sb.tile([P, 4, N], F32, name=f"expo{h}", align_bytes=64) for h in range(HALVES)]
        for turn, s in enumerate(SIDE_ORDER):
            grouped = sb.tile([P, N, 4], BF16, name=f"grouped{s}", tag=f"stage{turn % 2}", align_bytes=64)
            dst = grouped[:].rearrange("p (c i) t -> p c t i", i=4)
            src = raw[s][:].rearrange("p t (c i) -> p c t i", i=4)
            if turn < SCALAR_CASTS:
                nc.scalar.activation(dst, src, ACT.Copy)
            else:
                nc.vector.tensor_copy(dst, src)
            w_codes = sb.tile([P, N], U32, name=f"w_codes{s}", align_bytes=64)
            w_bytes = sb.tile([P, N], U8, name=f"w_bytes{s}", align_bytes=64)
            nc.vector.quantize_mx(
                out=w_codes[:].bitcast(FP8X4), scales=w_bytes[:], in_=grouped[:].rearrange("p m t -> p (m t)")
            )
            for h in range(HALVES):
                cols = slice(h * P, (h + 1) * P)
                nc.tensor.matmul_mx(
                    out=logits[h][s // 2][:, s % 2, :],
                    lhsT=x_codes[:, cols].bitcast(FP8X4),
                    lhsT_scale=x_bytes[:, cols],
                    rhs=w_codes[:].bitcast(FP8X4),
                    rhs_scale=w_bytes[:],
                    start=True,
                    stop=True,
                )
                nc.scalar.activation(expo[h][:, s, :], logits[h][s // 2][:, s % 2, :], ACT.Exp)

        picked = sb.tile([P, S], F32, name="picked", tag="stage1", align_bytes=64)
        nc.vector.tensor_copy(picked[:], truth_table[:].indirect(offsets[:]))
        turned = ps.tile([P, HALVES, P], F32, name="turned")
        for h in range(HALVES):
            nc.tensor.transpose(turned[:, h, :], picked[:, h * P : (h + 1) * P], ident[:])

        capped = sb.tile([P, HALVES, 4, N], F32, name="capped", tag="wide", align_bytes=64)
        for h in range(HALVES):
            nc.vector.tensor_scalar(capped[:, h], expo[h][:], EXP_CAP, None, ALU.min)

        g = sb.tile([P, HALVES, 4], F32, name="g")
        nc.vector.tensor_copy(g[:], turned[:, :, 0 : 4 * ROW_STEP : ROW_STEP])
        g_sum = sb.tile([P, HALVES, 2], F32, name="g_sum")
        nc.vector.tensor_tensor(g_sum[:], g[:, :, 0:2], g[:, :, 2:4], ALU.add)
        g_area = sb.tile([P, HALVES], F32, name="g_area")
        nc.vector.tensor_tensor(g_area[:], g_sum[:, :, 0], g_sum[:, :, 1], ALU.mult)

        soft = [sb.tile([P, 4, N], F32, name=f"soft{h}", align_bytes=64) for h in range(HALVES)]
        pred = [sb.tile([P, 4, N], F32, name=f"pred{h}", align_bytes=64) for h in range(HALVES)]
        low = [sb.tile([P, 2, N], F32, name=f"low{h}", align_bytes=64) for h in range(HALVES)]
        for h in range(HALVES):
            for end in (1, 0):
                pair = slice(2 * end, 2 * end + 2)
                nc.scalar.activation(soft[h][:, pair, :], capped[:, h, pair, :], ACT.Ln, bias=1.0)

        union, hull, overlap = [], [], []
        for h in range(HALVES):
            for end in (1, 0):
                pair = slice(2 * end, 2 * end + 2)
                nc.vector.tensor_tensor(pred[h][:, pair, :], logits[h][end][:], soft[h][:, pair, :], ALU.max)
                if end == 1:
                    for axis in range(2):
                        nc.vector.tensor_scalar(
                            low[h][:, axis, :], pred[h][:, 2 + axis, :], g[:, h, 2 + axis : 3 + axis], None, ALU.min
                        )
            spans = sb.tile([P, 3, 2, N], F32, name=f"spans{h}", align_bytes=64)
            areas = sb.tile([P, 3, N], F32, name=f"areas{h}", align_bytes=64)
            union.append(ps.tile([P, P], F32, name=f"union{h}"))
            hull.append(ps.tile([P, P], F32, name=f"hull{h}", tag=f"logits{h}1"))
            overlap.append(ps.tile([P, P], F32, name=f"overlap{h}", tag=f"logits{h}0"))
            nc.tensor.matmul(
                union[h][:],
                lhsT=g_area[:, h : h + 1].to_broadcast([P, P]),
                rhs=ident[:],
                is_transpose=True,
                start=True,
                stop=False,
            )
            nc.vector.tensor_tensor(spans[:, 1], pred[h][:, 0:2, :], pred[h][:, 2:4, :], ALU.add)
            for axis in range(2):
                nc.vector.scalar_tensor_tensor(
                    spans[:, 0, axis, :],
                    pred[h][:, axis, :],
                    g[:, h, axis : axis + 1],
                    low[h][:, axis, :],
                    ALU.min,
                    ALU.add,
                )
            nc.vector.tensor_tensor(areas[:, 1, :], spans[:, 1, 0, :], spans[:, 1, 1, :], ALU.mult)
            nc.tensor.matmul(union[h][:], lhsT=areas[:, 1, :], rhs=ident[:], is_transpose=True, start=False, stop=False)
            nc.vector.scalar_tensor_tensor(
                areas[:, 0, :], spans[:, 0, 0, :], -1.0, spans[:, 0, 1, :], ALU.mult, ALU.mult
            )
            nc.tensor.matmul(union[h][:], lhsT=areas[:, 0, :], rhs=ident[:], is_transpose=True, start=False, stop=True)
            nc.tensor.transpose(overlap[h][:], areas[:, 0, :], ident[:])
            for axis in range(2):
                nc.vector.scalar_tensor_tensor(
                    spans[:, 2, axis, :],
                    spans[:, 1, axis, :],
                    g_sum[:, h, axis : axis + 1],
                    spans[:, 0, axis, :],
                    ALU.add,
                    ALU.subtract,
                )
            nc.vector.tensor_tensor(areas[:, 2, :], spans[:, 2, 0, :], spans[:, 2, 1, :], ALU.mult)
            nc.tensor.transpose(hull[h][:], areas[:, 2, :], ident[:])

        ratio = sb.tile([P, HALVES, 2, P], F32, name="ratio", tag="spans1", align_bytes=64)
        for h in range(HALVES):
            root = sb.tile([P, 2, P], F32, name=f"root{h}", align_bytes=64)
            recip = sb.tile([P, 2, P], F32, name=f"recip{h}", align_bytes=64)
            nc.scalar.activation(root[:, 0, :], union[h][:], ACT.Abs_reciprocal_sqrt)
            nc.scalar.activation(recip[:, 0, :], root[:, 0, :], ACT.Square)
            nc.scalar.activation(root[:, 1, :], hull[h][:], ACT.Abs_reciprocal_sqrt)
            nc.scalar.activation(recip[:, 1, :], root[:, 1, :], ACT.Square)
            nc.vector.tensor_tensor(ratio[:, h, 0, :], overlap[h][:], recip[:, 0, :], ALU.mult)
            nc.vector.scalar_tensor_tensor(ratio[:, h, 1, :], union[h][:], -1.0, recip[:, 1, :], ALU.mult, ALU.mult)
            loss = sb.tile([P, P], F32, name=f"loss{h}", align_bytes=64)
            nc.vector.scalar_tensor_tensor(loss[:], ratio[:, h, 1, :], 2.0, ratio[:, h, 0, :], ALU.add, ALU.add)
            nc.sync.dma_start(out[:, h * P : (h + 1) * P], loss[:])
